import numpy as np
import ml_dtypes


def mxq(x, axis, fmt="e4m3"):
    dtype, down = {"e4m3": (ml_dtypes.float8_e4m3fn, 7), "e5m2": (ml_dtypes.float8_e5m2, 14)}[fmt]
    v = np.moveaxis(np.asarray(x, np.float32).astype(ml_dtypes.bfloat16).astype(np.float64), axis, -1)
    blocks = v.reshape(v.shape[:-1] + (-1, 32))
    amax = np.abs(blocks).max(-1, keepdims=True)
    byte = np.maximum(np.where(amax > 0, np.frexp(amax)[1] - 1 + 127, 0) - down, 1)
    scale = np.exp2(byte - 127.0)
    codes = (blocks / scale).astype(np.float32).astype(dtype).astype(np.float64)
    return np.moveaxis((codes * scale).reshape(v.shape), -1, axis)


WIDE = False


def mx_kscale(k):
    if not WIDE:
        return np.ones(k)
    levels = np.array([10, -10, 5, -5, 0])
    if k % 512:
        return np.exp2(np.random.permutation(np.resize(levels, k // 32))).repeat(32)
    a = np.empty((k // 512, 16))
    for p in range(k // 512):
        a[p, :8] = np.random.permutation(np.resize(levels, 8))
        for g in range(8):
            far = levels[np.abs(levels - a[p, g]) >= 10]
            a[p, g + 8] = far[np.random.randint(len(far))]
    return np.exp2(a.ravel()).repeat(32)


def f64(x):
    return np.asarray(x).astype(np.float64)


def striped8(idx):
    return np.asarray(idx).reshape(8, -1, 16).transpose(0, 2, 1).reshape(128, -1).astype(np.uint16)


def unstriped8(offs):
    return offs.reshape(8, 16, -1).transpose(0, 2, 1).reshape(8, -1).astype(np.int64)


def pick8(x, idx, run):
    r = np.arange(len(x))
    return x[r[:, None], idx[r % (8 * run) // run]]


E2M1 = np.array([0.0, 0.5, 1.0, 1.5, 2.0, 3.0, 4.0, 6.0, -0.0, -0.5, -1.0, -1.5, -2.0, -3.0, -4.0, -6.0])


def pack_weight(w, fmt):
    k, n = w.shape
    w = f64(np.asarray(w, np.float32).astype(ml_dtypes.bfloat16)).reshape(k // 32, 32, n)
    amax = np.abs(w).max(1)
    if fmt == "e4m3":
        byte = np.frexp(amax)[1] - 1 + 127 - 7
    else:
        mant, ex = np.frexp(amax / 6.0)
        byte = np.where(mant > 0.5, ex, ex - 1) + 127
    byte = np.clip(np.where(amax > 0, byte, 1), 1, 254)
    scaled = (w * np.exp2(127.0 - byte)[:, None, :]).reshape(k, n).astype(np.float32)
    by_word = np.ascontiguousarray(scaled.reshape(k // 512, 128, 4, n).transpose(0, 1, 3, 2))
    if fmt == "e4m3":
        words = by_word.astype(ml_dtypes.float8_e4m3fn).view(np.uint8)
    else:
        c = by_word.astype(ml_dtypes.float4_e2m1fn).view(np.uint8) & 0xF
        words = (c[..., 0::2] | (c[..., 1::2] << 4)).reshape(k // 512, 128, 2 * n)
    return np.ascontiguousarray(words), np.ascontiguousarray(byte.astype(np.uint8).reshape(k // 512, 16, n))


def unpack_weight(words, scales, fmt):
    g, _, n = scales.shape
    words = np.ascontiguousarray(words).reshape(g, 128, n, -1)
    if fmt == "e4m3":
        vals = words.view(ml_dtypes.float8_e4m3fn).astype(np.float64)
    else:
        nib = np.empty((g, 128, n, 4), np.uint8)
        nib[..., 0::2] = words & 0xF
        nib[..., 1::2] = words >> 4
        vals = E2M1[nib]
    vals = vals * np.repeat(np.exp2(scales.astype(np.float64) - 127.0), 8, axis=1)[..., None]
    return vals.transpose(0, 1, 3, 2).reshape(g * 512, n)


def bf(x):
    return np.asarray(x, np.float32).astype(ml_dtypes.bfloat16)


def planes(Y):
    r, m = Y.shape
    b = f64(bf(Y)).reshape(r // 32, 32, m)
    amax = np.abs(b).max(1)
    byte = np.clip(np.where(amax > 0, np.frexp(amax)[1] - 1 + 127 - 7, 1), 1, 254)
    codes = (b * np.exp2(127.0 - byte)[:, None, :]).reshape(r, m).astype(np.float32).astype(ml_dtypes.float8_e4m3fn).view(np.uint8)
    words = codes.reshape(r // 512, 128, 4, m).transpose(0, 1, 3, 2)
    return np.ascontiguousarray(words), np.ascontiguousarray(byte.astype(np.uint8).reshape(r // 512, 16, m))


K, T, J, L, N = 512, 1024, 512, 512, 512


def setup_inputs():
    n = np.random.standard_normal
    idx = np.stack([np.random.permutation(T)[:J] for _ in range(8)])
    fk = mx_kscale(K)
    fl = mx_kscale(L)
    wp = pack_weight(n((K, N)) * 1 / np.sqrt(K) * fk[:, None], "e4m3")
    cxp = pack_weight(n((L, J)) / fl[:, None], "e2m1")
    wcp = pack_weight(n((L, N)) * 1 / np.sqrt(L) * fl[:, None], "e4m3")
    return {
        "xf": (n((K, T))).astype(np.float32),
        "fk": (np.random.uniform(0.5, 2.0, (K, 1)) / fk[:, None]).astype(np.float32),
        "w_words": wp[0],
        "w_scales": wp[1],
        "cx_words": cxp[0],
        "cx_scales": cxp[1],
        "wc_words": wcp[0],
        "wc_scales": wcp[1],
        "offs": striped8(idx),
    }


def reference(xf, fk, w_words, w_scales, cx_words, cx_scales, wc_words, wc_scales, offs):
    idx = unstriped8(offs)
    wu = unpack_weight(w_words, w_scales, "e4m3")
    cxu = unpack_weight(cx_words, cx_scales, "e2m1")
    wcu = unpack_weight(wc_words, wc_scales, "e4m3")
    xs = pick8(f64(xf), idx, 64) * f64(fk)
    xsq = mxq(xs, 0, "e4m3")
    p = wu.T @ xsq
    q = wcu.T @ cxu
    y = np.maximum(p, 0.0) + q
    words, scales = planes(y)
    return y, words, scales

@@ -1,0 +1,199 @@
+from contextlib import ExitStack
+
+import concourse.mybir as mybir
+
+K, T, J, L, N = 512, 1024, 512, 512, 512
+FLOPS = 2 * K * N * J + 2 * L * N * J
+
+F32 = mybir.dt.float32
+BF16 = mybir.dt.bfloat16
+I32 = mybir.dt.int32
+U32 = mybir.dt.uint32
+U16 = mybir.dt.uint16
+U8 = mybir.dt.uint8
+FP8X4 = mybir.dt.float8_e4m3fn_x4
+FP4X4 = mybir.dt.float4_e2m1fn_x4
+COPY = mybir.ActivationFunctionType.Copy
+MAX = mybir.AluOpType.max
+ADD = mybir.AluOpType.add
+
+P = 128
+PACK = 4
+HALF = 256
+CHUNK = 128
+NCHUNK = J // CHUNK
+
+
+def load_scale_rows(queue, plane, scales):
+    for quad in range(4):
+        rows = scales[0, 4 * quad : 4 * quad + 4, :].bitcast(I32)
+        queue.dma_start(
+            out=plane[32 * quad : 32 * quad + 32, :].bitcast(I32),
+            in_=rows.unsqueeze(0).broadcast_to([8, 4, rows.shape[1]]),
+        )
+
+
+def tile_list_group_picks_and_context_pl_kernel(
+    tc, xf, fk, w_words, w_scales, cx_words, cx_scales, wc_words, wc_scales, offs, out_0, out_1, out_2
+):
+    nc = tc.nc
+    with ExitStack() as ctx:
+        sb = ctx.enter_context(tc.tile_pool(name="sb", bufs=1))
+        ps = ctx.enter_context(tc.psum_pool(name="ps", bufs=1))
+
+        offsets = sb.tile([P, J // 16], U16, name="offsets")
+        planes = [sb.tile([P, T], F32, name=f"plane{t}") for t in range(PACK)]
+        factor = sb.tile([P, PACK], F32, name="factor")
+        w_raw = sb.tile([P, N], U32, name="w_raw", align_bytes=64)
+        wc_raw = sb.tile([P, N], U32, name="wc_raw", align_bytes=64)
+        cx_codes = sb.tile([P, 2 * J], U8, name="cx_codes", align_bytes=64)
+        cx_plane = sb.tile([P, J], U8, name="cx_plane", align_bytes=64)
+        scale_raw = sb.tile([P, 2 * N], U8, name="scale_raw", align_bytes=64)
+
+        xf_rows = xf.rearrange("(p t) c -> t p c", t=PACK)
+        nc.sync.dma_start(out=planes[0][:], in_=xf_rows[0])
+        nc.sync.dma_start(offsets[:], offs)
+        for t in range(1, PACK):
+            nc.sync.dma_start(out=planes[t][:], in_=xf_rows[t])
+        nc.sync.dma_start(out=w_raw[:].bitcast(I32), in_=w_words[0].rearrange("p n t -> p (n t)").bitcast(I32))
+        nc.sync.dma_start(out=wc_raw[:].bitcast(I32), in_=wc_words[0].rearrange("p n t -> p (n t)").bitcast(I32))
+        nc.sync.dma_start(out=cx_codes[:].bitcast(I32), in_=cx_words[0].bitcast(I32))
+        load_scale_rows(nc.scalar, scale_raw[:, 0:N], w_scales)
+        load_scale_rows(nc.scalar, scale_raw[:, N : 2 * N], wc_scales)
+        nc.gpsimd.dma_start(out=factor[:], in_=fk.rearrange("(p t) o -> p (t o)", t=PACK))
+        load_scale_rows(nc.gpsimd, cx_plane[:, :], cx_scales)
+
+        scale_dealt = sb.tile([P, PACK, 2, P], U8, name="scale_dealt", align_bytes=64)
+        nc.vector.tensor_copy(
+            out=scale_dealt[:].rearrange("p t a (c i) -> p (a c) t i", i=16),
+            in_=scale_raw[:].rearrange("p (c i t) -> p c t i", i=16, t=PACK),
+        )
+
+        picked = [sb.tile([P, J], F32, name=f"picked{t}") for t in range(PACK - 1)]
+        picked_last = [sb.tile([P, HALF], F32, name=f"picked_last{h}") for h in range(2)]
+        pairs = [sb.tile([P, 2, HALF, 2], BF16, name=f"pairs{h}", align_bytes=64) for h in range(2)]
+        for t in range(PACK - 1):
+            nc.vector.tensor_copy(out=picked[t][:], in_=planes[t][:].indirect(offsets[:]))
+            for h in range(2):
+                nc.scalar.activation(
+                    out=pairs[h][:, t // 2, :, t % 2],
+                    in_=picked[t][:, h * HALF : (h + 1) * HALF],
+                    func=COPY,
+                    scale=factor[:, t : t + 1],
+                )
+        for h in range(2):
+            cols = HALF // 16
+            nc.vector.tensor_copy(
+                out=picked_last[h][:], in_=planes[PACK - 1][:].indirect(offsets[:, h * cols : (h + 1) * cols])
+            )
+            nc.scalar.activation(
+                out=pairs[h][:, 1, :, 1], in_=picked_last[h][:], func=COPY, scale=factor[:, PACK - 1 : PACK]
+            )
+
+        w_dealt = sb.tile([P, PACK, P], U32, name="w_dealt", align_bytes=64)
+        wc_dealt = sb.tile([P, PACK, P], U32, name="wc_dealt", align_bytes=64)
+
+        def deal(dealt, raw):
+            nc.vector.tensor_copy(
+                out=dealt[:].bitcast(I32).rearrange("p t (c i) -> p c t i", i=4),
+                in_=raw[:].bitcast(I32).rearrange("p (c i t) -> p c t i", i=4, t=PACK),
+            )
+
+        xs = [sb.tile([P, HALF * PACK], BF16, name=f"xs{h}", align_bytes=64) for h in range(2)]
+        xs_codes = [sb.tile([P, HALF], U32, name=f"xs_codes{h}", align_bytes=64) for h in range(2)]
+        xs_plane = [sb.tile([P, HALF], U8, name=f"xs_plane{h}", align_bytes=64) for h in range(2)]
+
+        def weave(h):
+            nc.vector.tensor_copy(
+                out=xs[h][:].bitcast(I32).rearrange("p (c i u) -> p c u i", i=2, u=2),
+                in_=pairs[h][:].rearrange("p u j e -> p (u j e)").bitcast(I32).rearrange("p (u c i) -> p c u i", u=2, i=2),
+            )
+
+        def quantise_xs(h):
+            nc.vector.quantize_mx(out=xs_codes[h][:].bitcast(FP8X4), scales=xs_plane[h][:], in_=xs[h][:])
+
+        deal(w_dealt, w_raw)
+        weave(0)
+        deal(wc_dealt, wc_raw)
+        quantise_xs(0)
+        weave(1)
+
+        q_bank = [ps.tile([P, PACK, CHUNK], F32, name=f"q_bank{c}") for c in range(NCHUNK)]
+        p_bank = [ps.tile([P, PACK, CHUNK], F32, name=f"p_bank{c}") for c in range(NCHUNK)]
+        q_sb = [sb.tile([P, PACK * CHUNK], F32, name=f"q_sb{c}") for c in range(NCHUNK)]
+
+        def q_product(c):
+            for t in range(PACK):
+                nc.tensor.matmul_mx(
+                    out=q_bank[c][:, t, :],
+                    lhsT=wc_dealt[:, t, :].bitcast(FP8X4),
+                    lhsT_scale=scale_dealt[:, t, 1, :],
+                    rhs=cx_codes[:, 2 * c * CHUNK : 2 * (c + 1) * CHUNK].bitcast(FP4X4),
+                    rhs_scale=cx_plane[:, c * CHUNK : (c + 1) * CHUNK],
+                    start=True,
+                    stop=True,
+                )
+            nc.scalar.copy(out=q_sb[c][:], in_=q_bank[c][:].rearrange("p t j -> p (t j)"))
+
+        def p_product(c):
+            h, cols = c // 2, slice((c % 2) * CHUNK, (c % 2 + 1) * CHUNK)
+            for t in range(PACK):
+                nc.tensor.matmul_mx(
+                    out=p_bank[c][:, t, :],
+                    lhsT=w_dealt[:, t, :].bitcast(FP8X4),
+                    lhsT_scale=scale_dealt[:, t, 0, :],
+                    rhs=xs_codes[h][:, cols].bitcast(FP8X4),
+                    rhs_scale=xs_plane[h][:, cols],
+                    start=True,
+                    stop=True,
+                )
+
+        q_product(0)
+        p_product(0)
+        quantise_xs(1)
+        for c in range(1, NCHUNK):
+            q_product(c)
+            p_product(c)
+
+        y = [sb.tile([P, PACK, CHUNK], F32, name=f"y{c}") for c in range(NCHUNK)]
+        y_bf = [sb.tile([P, CHUNK * PACK], BF16, name=f"y_bf{c}", align_bytes=64) for c in range(NCHUNK)]
+        y_codes = sb.tile([P, J], U32, name="y_codes", align_bytes=64)
+        y_plane = sb.tile([P, J], U8, name="y_plane", align_bytes=64)
+        out_rows = out_0.rearrange("(p t) j -> p t j", t=PACK)
+        out_words = out_1[0].rearrange("p j t -> p (j t)").bitcast(I32)
+
+        def round_y(engine_copy, c):
+            engine_copy(
+                out=y_bf[c][:].rearrange("p (c i t) -> p c t i", i=2, t=PACK),
+                in_=y[c][:].rearrange("p t (c i) -> p c t i", i=2),
+            )
+
+        def quantise_y(c):
+            cols = slice(c * CHUNK, (c + 1) * CHUNK)
+            nc.vector.quantize_mx(out=y_codes[:, cols].bitcast(FP8X4), scales=y_plane[:, cols], in_=y_bf[c][:])
+
+        for c in range(NCHUNK):
+            nc.vector.scalar_tensor_tensor(
+                out=y[c][:].rearrange("p t j -> p (t j)"),
+                in0=p_bank[c][:].rearrange("p t j -> p (t j)"),
+                scalar=0.0,
+                in1=q_sb[c][:],
+                op0=MAX,
+                op1=ADD,
+            )
+            nc.sync.dma_start(out=out_rows[:, :, c * CHUNK : (c + 1) * CHUNK], in_=y[c][:])
+            if c < NCHUNK - 1:
+                round_y(nc.scalar.copy, c)
+        quantise_y(0)
+        quantise_y(1)
+        nc.sync.dma_start(out=out_words[:, 0:HALF], in_=y_codes[:, 0:HALF].bitcast(I32))
+        round_y(nc.vector.tensor_copy, NCHUNK - 1)
+        quantise_y(2)
+        quantise_y(3)
+        nc.sync.dma_start(out=out_words[:, HALF:J], in_=y_codes[:, HALF:J].bitcast(I32))
+        for quad in range(4):
+            queue = nc.scalar if quad % 2 == 0 else nc.sync
+            queue.dma_start(
+                out=out_2[0, 4 * quad : 4 * quad + 4, :].bitcast(I32),
+                in_=y_plane[32 * quad : 32 * quad + 4, :].bitcast(I32),
+            )

@@ -24,15 +24,6 @@ CHUNK = 128
 NCHUNK = J // CHUNK
 
 
-def load_scale_rows(queue, plane, scales):
-    for quad in range(4):
-        rows = scales[0, 4 * quad : 4 * quad + 4, :].bitcast(I32)
-        queue.dma_start(
-            out=plane[32 * quad : 32 * quad + 32, :].bitcast(I32),
-            in_=rows.unsqueeze(0).broadcast_to([8, 4, rows.shape[1]]),
-        )
-
-
 def tile_list_group_picks_and_context_pl_kernel(
     tc, xf, fk, w_words, w_scales, cx_words, cx_scales, wc_words, wc_scales, offs, out_0, out_1, out_2
 ):
@@ -44,35 +35,60 @@ def tile_list_group_picks_and_context_pl_kernel(
         offsets = sb.tile([P, J // 16], U16, name="offsets")
         planes = [sb.tile([P, T], F32, name=f"plane{t}") for t in range(PACK)]
         factor = sb.tile([P, PACK], F32, name="factor")
-        w_raw = sb.tile([P, N], U32, name="w_raw", align_bytes=64)
-        wc_raw = sb.tile([P, N], U32, name="wc_raw", align_bytes=64)
+        wc_raw = sb.tile([P, N], U32, name="wc_raw", tag="raw_words", align_bytes=64)
         cx_codes = sb.tile([P, 2 * J], U8, name="cx_codes", align_bytes=64)
-        cx_plane = sb.tile([P, J], U8, name="cx_plane", align_bytes=64)
-        scale_raw = sb.tile([P, 2 * N], U8, name="scale_raw", align_bytes=64)
+        scale_quads = sb.tile([P, 8, 2, N], U8, name="scale_quads", align_bytes=64)
+        scale_rows = sb.tile([P, 2, N], U8, name="scale_rows", align_bytes=64)
+        nc.vector.memset(scale_quads[:, 4:8, 1, :].bitcast(I32), 0)
+        nc.vector.memset(scale_rows[:].rearrange("p a n -> p (a n)").bitcast(I32), 0)
+
+        warm = sb.tile([P, 2], F32, name="warm")
+        nc.vector.memset(warm[:, 0:1], 0.0)
+        nc.scalar.activation(out=warm[:, 1:2], in_=warm[:, 0:1], func=COPY)
 
         xf_rows = xf.rearrange("(p t) c -> t p c", t=PACK)
         nc.sync.dma_start(out=planes[0][:], in_=xf_rows[0])
         nc.sync.dma_start(offsets[:], offs)
-        for t in range(1, PACK):
-            nc.sync.dma_start(out=planes[t][:], in_=xf_rows[t])
-        nc.sync.dma_start(out=w_raw[:].bitcast(I32), in_=w_words[0].rearrange("p n t -> p (n t)").bitcast(I32))
+        nc.sync.dma_start(out=factor[:], in_=fk.rearrange("(p t) o -> p (t o)", t=PACK))
         nc.sync.dma_start(out=wc_raw[:].bitcast(I32), in_=wc_words[0].rearrange("p n t -> p (n t)").bitcast(I32))
+        nc.sync.dma_start(out=planes[1][:], in_=xf_rows[1])
+        nc.sync.dma_start(out=planes[2][:], in_=xf_rows[2])
         nc.sync.dma_start(out=cx_codes[:].bitcast(I32), in_=cx_words[0].bitcast(I32))
-        load_scale_rows(nc.scalar, scale_raw[:, 0:N], w_scales)
-        load_scale_rows(nc.scalar, scale_raw[:, N : 2 * N], wc_scales)
-        nc.gpsimd.dma_start(out=factor[:], in_=fk.rearrange("(p t) o -> p (t o)", t=PACK))
-        load_scale_rows(nc.gpsimd, cx_plane[:, :], cx_scales)
+        nc.sync.dma_start(out=planes[3][:], in_=xf_rows[3])
+        for scales, row, slot in ((wc_scales, 0, 0), (cx_scales, 0, 1), (w_scales, 4, 0)):
+            nc.scalar.dma_start(
+                out=scale_quads[0:P:32, row : row + 4, slot, :].bitcast(I32),
+                in_=scales[0].bitcast(I32).rearrange("(q r) c -> q r c", r=4),
+            )
+        for quad in range(4):
+            nc.scalar.dma_start(
+                out=scale_rows[32 * quad : 32 * quad + 8, :, :].rearrange("p a n -> p (a n)").bitcast(I32),
+                in_=scale_quads[32 * quad : 32 * quad + 1, :, :, :].rearrange("p r a n -> p r (a n)").bitcast(I32),
+            )
 
-        scale_dealt = sb.tile([P, PACK, 2, P], U8, name="scale_dealt", align_bytes=64)
-        nc.vector.tensor_copy(
-            out=scale_dealt[:].rearrange("p t a (c i) -> p (a c) t i", i=16),
-            in_=scale_raw[:].rearrange("p (c i t) -> p c t i", i=16, t=PACK),
-        )
+        w_dealt = sb.tile([P, PACK, P], U32, name="w_dealt", align_bytes=64)
+        wc_dealt = sb.tile([P, PACK, P], U32, name="wc_dealt", align_bytes=64)
+        scale_dealt = sb.tile([P, PACK, P], U8, name="scale_dealt", align_bytes=64)
+
+        def deal_words(dealt, raw):
+            nc.vector.tensor_copy(
+                out=dealt[:].bitcast(I32).rearrange("p t (c i) -> p c t i", i=4),
+                in_=raw[:].bitcast(I32).rearrange("p (c i t) -> p c t i", i=4, t=PACK),
+            )
+
+        def deal_scales():
+            nc.vector.tensor_copy(
+                out=scale_dealt[:].rearrange("p t (c i) -> p c t i", i=16),
+                in_=scale_rows[:, 0, :].rearrange("p (c i t) -> p c t i", i=16, t=PACK),
+            )
 
         picked = [sb.tile([P, J], F32, name=f"picked{t}") for t in range(PACK - 1)]
-        picked_last = [sb.tile([P, HALF], F32, name=f"picked_last{h}") for h in range(2)]
-        pairs = [sb.tile([P, 2, HALF, 2], BF16, name=f"pairs{h}", align_bytes=64) for h in range(2)]
-        for t in range(PACK - 1):
+        picked_last = [sb.tile([P, HALF], F32, name=f"picked_last{h}", tag=f"last{h}", align_bytes=64) for h in range(2)]
+        pairs = [sb.tile([P, 2, HALF, 2], BF16, name=f"pairs{h}", tag=f"pairs{h}", align_bytes=64) for h in range(2)]
+        q_bank = [ps.tile([P, PACK, CHUNK], F32, name=f"q_bank{c}") for c in range(NCHUNK)]
+        p_bank = [ps.tile([P, PACK, CHUNK], F32, name=f"p_bank{c}") for c in range(NCHUNK)]
+
+        def pick(t):
             nc.vector.tensor_copy(out=picked[t][:], in_=planes[t][:].indirect(offsets[:]))
             for h in range(2):
                 nc.scalar.activation(
@@ -81,6 +97,35 @@ def tile_list_group_picks_and_context_pl_kernel(
                     func=COPY,
                     scale=factor[:, t : t + 1],
                 )
+
+        def q_product(c):
+            for t in range(PACK):
+                nc.tensor.matmul_mx(
+                    out=q_bank[c][:, t, :],
+                    lhsT=wc_dealt[:, t, :].bitcast(FP8X4),
+                    lhsT_scale=scale_dealt[:, t, :],
+                    rhs=cx_codes[:, 2 * c * CHUNK : 2 * (c + 1) * CHUNK].bitcast(FP4X4),
+                    rhs_scale=scale_rows[:, 1, c * CHUNK : (c + 1) * CHUNK],
+                    start=True,
+                    stop=True,
+                )
+
+        q_sb = []
+
+        def q_copy(c, tag):
+            q_chunk = sb.tile([P, PACK * CHUNK], F32, name=f"q_sb{c}", tag=tag, align_bytes=64)
+            q_sb.append(q_chunk)
+            nc.scalar.copy(out=q_chunk[:], in_=q_bank[c][:].rearrange("p t j -> p (t j)"))
+
+        pick(0)
+        deal_words(wc_dealt, wc_raw)
+        w_raw = sb.tile([P, N], U32, name="w_raw", tag="raw_words", align_bytes=64)
+        nc.sync.dma_start(out=w_raw[:].bitcast(I32), in_=w_words[0].rearrange("p n t -> p (n t)").bitcast(I32))
+        pick(1)
+        deal_scales()
+        pick(2)
+        for c in range(NCHUNK):
+            q_product(c)
         for h in range(2):
             cols = HALF // 16
             nc.vector.tensor_copy(
@@ -89,15 +134,8 @@ def tile_list_group_picks_and_context_pl_kernel(
             nc.scalar.activation(
                 out=pairs[h][:, 1, :, 1], in_=picked_last[h][:], func=COPY, scale=factor[:, PACK - 1 : PACK]
             )
-
-        w_dealt = sb.tile([P, PACK, P], U32, name="w_dealt", align_bytes=64)
-        wc_dealt = sb.tile([P, PACK, P], U32, name="wc_dealt", align_bytes=64)
-
-        def deal(dealt, raw):
-            nc.vector.tensor_copy(
-                out=dealt[:].bitcast(I32).rearrange("p t (c i) -> p c t i", i=4),
-                in_=raw[:].bitcast(I32).rearrange("p (c i t) -> p c t i", i=4, t=PACK),
-            )
+        q_copy(0, "last0")
+        q_copy(1, "last1")
 
         xs = [sb.tile([P, HALF * PACK], BF16, name=f"xs{h}", align_bytes=64) for h in range(2)]
         xs_codes = [sb.tile([P, HALF], U32, name=f"xs_codes{h}", align_bytes=64) for h in range(2)]
@@ -112,28 +150,12 @@ def tile_list_group_picks_and_context_pl_kernel(
         def quantise_xs(h):
             nc.vector.quantize_mx(out=xs_codes[h][:].bitcast(FP8X4), scales=xs_plane[h][:], in_=xs[h][:])
 
-        deal(w_dealt, w_raw)
         weave(0)
-        deal(wc_dealt, wc_raw)
+        q_copy(2, "pairs0")
+        deal_words(w_dealt, w_raw)
         quantise_xs(0)
         weave(1)
-
-        q_bank = [ps.tile([P, PACK, CHUNK], F32, name=f"q_bank{c}") for c in range(NCHUNK)]
-        p_bank = [ps.tile([P, PACK, CHUNK], F32, name=f"p_bank{c}") for c in range(NCHUNK)]
-        q_sb = [sb.tile([P, PACK * CHUNK], F32, name=f"q_sb{c}") for c in range(NCHUNK)]
-
-        def q_product(c):
-            for t in range(PACK):
-                nc.tensor.matmul_mx(
-                    out=q_bank[c][:, t, :],
-                    lhsT=wc_dealt[:, t, :].bitcast(FP8X4),
-                    lhsT_scale=scale_dealt[:, t, 1, :],
-                    rhs=cx_codes[:, 2 * c * CHUNK : 2 * (c + 1) * CHUNK].bitcast(FP4X4),
-                    rhs_scale=cx_plane[:, c * CHUNK : (c + 1) * CHUNK],
-                    start=True,
-                    stop=True,
-                )
-            nc.scalar.copy(out=q_sb[c][:], in_=q_bank[c][:].rearrange("p t j -> p (t j)"))
+        q_copy(3, "pairs1")
 
         def p_product(c):
             h, cols = c // 2, slice((c % 2) * CHUNK, (c % 2 + 1) * CHUNK)
@@ -141,18 +163,16 @@ def tile_list_group_picks_and_context_pl_kernel(
                 nc.tensor.matmul_mx(
                     out=p_bank[c][:, t, :],
                     lhsT=w_dealt[:, t, :].bitcast(FP8X4),
-                    lhsT_scale=scale_dealt[:, t, 0, :],
+                    lhsT_scale=scale_dealt[4:P, t, :],
                     rhs=xs_codes[h][:, cols].bitcast(FP8X4),
                     rhs_scale=xs_plane[h][:, cols],
                     start=True,
                     stop=True,
                 )
 
-        q_product(0)
         p_product(0)
         quantise_xs(1)
         for c in range(1, NCHUNK):
-            q_product(c)
             p_product(c)
 
         y = [sb.tile([P, PACK, CHUNK], F32, name=f"y{c}") for c in range(NCHUNK)]

from contextlib import ExitStack

import concourse.mybir as mybir

K, T, J, L, N = 512, 1024, 512, 512, 512
FLOPS = 2 * K * N * J + 2 * L * N * J

F32 = mybir.dt.float32
BF16 = mybir.dt.bfloat16
I32 = mybir.dt.int32
U32 = mybir.dt.uint32
U16 = mybir.dt.uint16
U8 = mybir.dt.uint8
FP8X4 = mybir.dt.float8_e4m3fn_x4
FP4X4 = mybir.dt.float4_e2m1fn_x4
COPY = mybir.ActivationFunctionType.Copy
MAX = mybir.AluOpType.max
ADD = mybir.AluOpType.add

P = 128
PACK = 4
HALF = 256
CHUNK = 128
NCHUNK = J // CHUNK


def tile_list_group_picks_and_context_pl_kernel(
    tc, xf, fk, w_words, w_scales, cx_words, cx_scales, wc_words, wc_scales, offs, out_0, out_1, out_2
):
    nc = tc.nc
    with ExitStack() as ctx:
        sb = ctx.enter_context(tc.tile_pool(name="sb", bufs=1))
        ps = ctx.enter_context(tc.psum_pool(name="ps", bufs=1))

        offsets = sb.tile([P, J // 16], U16, name="offsets")
        planes = [sb.tile([P, T], F32, name=f"plane{t}") for t in range(PACK)]
        factor = sb.tile([P, PACK], F32, name="factor")
        wc_raw = sb.tile([P, N], U32, name="wc_raw", tag="raw_words", align_bytes=64)
        cx_codes = sb.tile([P, 2 * J], U8, name="cx_codes", align_bytes=64)
        scale_quads = sb.tile([P, 8, 2, N], U8, name="scale_quads", align_bytes=64)
        scale_rows = sb.tile([P, 2, N], U8, name="scale_rows", align_bytes=64)
        nc.vector.memset(scale_quads[:, 4:8, 1, :].bitcast(I32), 0)
        nc.vector.memset(scale_rows[:].rearrange("p a n -> p (a n)").bitcast(I32), 0)

        warm = sb.tile([P, 2], F32, name="warm")
        nc.vector.memset(warm[:, 0:1], 0.0)
        nc.scalar.activation(out=warm[:, 1:2], in_=warm[:, 0:1], func=COPY)

        xf_rows = xf.rearrange("(p t) c -> t p c", t=PACK)
        nc.sync.dma_start(out=planes[0][:], in_=xf_rows[0])
        nc.sync.dma_start(offsets[:], offs)
        nc.sync.dma_start(out=factor[:], in_=fk.rearrange("(p t) o -> p (t o)", t=PACK))
        nc.sync.dma_start(out=wc_raw[:].bitcast(I32), in_=wc_words[0].rearrange("p n t -> p (n t)").bitcast(I32))
        nc.sync.dma_start(out=planes[1][:], in_=xf_rows[1])
        nc.sync.dma_start(out=planes[2][:], in_=xf_rows[2])
        nc.sync.dma_start(out=cx_codes[:].bitcast(I32), in_=cx_words[0].bitcast(I32))
        nc.sync.dma_start(out=planes[3][:], in_=xf_rows[3])
        for scales, row, slot in ((wc_scales, 0, 0), (cx_scales, 0, 1), (w_scales, 4, 0)):
            nc.scalar.dma_start(
                out=scale_quads[0:P:32, row : row + 4, slot, :].bitcast(I32),
                in_=scales[0].bitcast(I32).rearrange("(q r) c -> q r c", r=4),
            )
        for quad in range(4):
            nc.scalar.dma_start(
                out=scale_rows[32 * quad : 32 * quad + 8, :, :].rearrange("p a n -> p (a n)").bitcast(I32),
                in_=scale_quads[32 * quad : 32 * quad + 1, :, :, :].rearrange("p r a n -> p r (a n)").bitcast(I32),
            )

        w_dealt = sb.tile([P, PACK, P], U32, name="w_dealt", align_bytes=64)
        wc_dealt = sb.tile([P, PACK, P], U32, name="wc_dealt", align_bytes=64)
        scale_dealt = sb.tile([P, PACK, P], U8, name="scale_dealt", align_bytes=64)

        def deal_words(dealt, raw):
            nc.vector.tensor_copy(
                out=dealt[:].bitcast(I32).rearrange("p t (c i) -> p c t i", i=4),
                in_=raw[:].bitcast(I32).rearrange("p (c i t) -> p c t i", i=4, t=PACK),
            )

        def deal_scales():
            nc.vector.tensor_copy(
                out=scale_dealt[:].rearrange("p t (c i) -> p c t i", i=16),
                in_=scale_rows[:, 0, :].rearrange("p (c i t) -> p c t i", i=16, t=PACK),
            )

        picked = [sb.tile([P, J], F32, name=f"picked{t}") for t in range(PACK - 1)]
        picked_last = [sb.tile([P, HALF], F32, name=f"picked_last{h}", tag=f"last{h}", align_bytes=64) for h in range(2)]
        pairs = [sb.tile([P, 2, HALF, 2], BF16, name=f"pairs{h}", tag=f"pairs{h}", align_bytes=64) for h in range(2)]
        q_bank = [ps.tile([P, PACK, CHUNK], F32, name=f"q_bank{c}") for c in range(NCHUNK)]
        p_bank = [ps.tile([P, PACK, CHUNK], F32, name=f"p_bank{c}") for c in range(NCHUNK)]

        def pick(t):
            nc.vector.tensor_copy(out=picked[t][:], in_=planes[t][:].indirect(offsets[:]))
            for h in range(2):
                nc.scalar.activation(
                    out=pairs[h][:, t // 2, :, t % 2],
                    in_=picked[t][:, h * HALF : (h + 1) * HALF],
                    func=COPY,
                    scale=factor[:, t : t + 1],
                )

        def q_product(c):
            for t in range(PACK):
                nc.tensor.matmul_mx(
                    out=q_bank[c][:, t, :],
                    lhsT=wc_dealt[:, t, :].bitcast(FP8X4),
                    lhsT_scale=scale_dealt[:, t, :],
                    rhs=cx_codes[:, 2 * c * CHUNK : 2 * (c + 1) * CHUNK].bitcast(FP4X4),
                    rhs_scale=scale_rows[:, 1, c * CHUNK : (c + 1) * CHUNK],
                    start=True,
                    stop=True,
                )

        q_sb = []

        def q_copy(c, tag):
            q_chunk = sb.tile([P, PACK * CHUNK], F32, name=f"q_sb{c}", tag=tag, align_bytes=64)
            q_sb.append(q_chunk)
            nc.scalar.copy(out=q_chunk[:], in_=q_bank[c][:].rearrange("p t j -> p (t j)"))

        pick(0)
        deal_words(wc_dealt, wc_raw)
        w_raw = sb.tile([P, N], U32, name="w_raw", tag="raw_words", align_bytes=64)
        nc.sync.dma_start(out=w_raw[:].bitcast(I32), in_=w_words[0].rearrange("p n t -> p (n t)").bitcast(I32))
        pick(1)
        deal_scales()
        pick(2)
        for c in range(NCHUNK):
            q_product(c)
        for h in range(2):
            cols = HALF // 16
            nc.vector.tensor_copy(
                out=picked_last[h][:], in_=planes[PACK - 1][:].indirect(offsets[:, h * cols : (h + 1) * cols])
            )
            nc.scalar.activation(
                out=pairs[h][:, 1, :, 1], in_=picked_last[h][:], func=COPY, scale=factor[:, PACK - 1 : PACK]
            )
        q_copy(0, "last0")
        q_copy(1, "last1")

        xs = [sb.tile([P, HALF * PACK], BF16, name=f"xs{h}", align_bytes=64) for h in range(2)]
        xs_codes = [sb.tile([P, HALF], U32, name=f"xs_codes{h}", align_bytes=64) for h in range(2)]
        xs_plane = [sb.tile([P, HALF], U8, name=f"xs_plane{h}", align_bytes=64) for h in range(2)]

        def weave(h):
            nc.vector.tensor_copy(
                out=xs[h][:].bitcast(I32).rearrange("p (c i u) -> p c u i", i=2, u=2),
                in_=pairs[h][:].rearrange("p u j e -> p (u j e)").bitcast(I32).rearrange("p (u c i) -> p c u i", u=2, i=2),
            )

        def quantise_xs(h):
            nc.vector.quantize_mx(out=xs_codes[h][:].bitcast(FP8X4), scales=xs_plane[h][:], in_=xs[h][:])

        weave(0)
        q_copy(2, "pairs0")
        deal_words(w_dealt, w_raw)
        quantise_xs(0)
        weave(1)
        q_copy(3, "pairs1")

        def p_product(c):
            h, cols = c // 2, slice((c % 2) * CHUNK, (c % 2 + 1) * CHUNK)
            for t in range(PACK):
                nc.tensor.matmul_mx(
                    out=p_bank[c][:, t, :],
                    lhsT=w_dealt[:, t, :].bitcast(FP8X4),
                    lhsT_scale=scale_dealt[4:P, t, :],
                    rhs=xs_codes[h][:, cols].bitcast(FP8X4),
                    rhs_scale=xs_plane[h][:, cols],
                    start=True,
                    stop=True,
                )

        p_product(0)
        quantise_xs(1)
        for c in range(1, NCHUNK):
            p_product(c)

        y = [sb.tile([P, PACK, CHUNK], F32, name=f"y{c}") for c in range(NCHUNK)]
        y_bf = [sb.tile([P, CHUNK * PACK], BF16, name=f"y_bf{c}", align_bytes=64) for c in range(NCHUNK)]
        y_codes = sb.tile([P, J], U32, name="y_codes", align_bytes=64)
        y_plane = sb.tile([P, J], U8, name="y_plane", align_bytes=64)
        out_rows = out_0.rearrange("(p t) j -> p t j", t=PACK)
        out_words = out_1[0].rearrange("p j t -> p (j t)").bitcast(I32)

        def round_y(engine_copy, c):
            engine_copy(
                out=y_bf[c][:].rearrange("p (c i t) -> p c t i", i=2, t=PACK),
                in_=y[c][:].rearrange("p t (c i) -> p c t i", i=2),
            )

        def quantise_y(c):
            cols = slice(c * CHUNK, (c + 1) * CHUNK)
            nc.vector.quantize_mx(out=y_codes[:, cols].bitcast(FP8X4), scales=y_plane[:, cols], in_=y_bf[c][:])

        for c in range(NCHUNK):
            nc.vector.scalar_tensor_tensor(
                out=y[c][:].rearrange("p t j -> p (t j)"),
                in0=p_bank[c][:].rearrange("p t j -> p (t j)"),
                scalar=0.0,
                in1=q_sb[c][:],
                op0=MAX,
                op1=ADD,
            )
            nc.sync.dma_start(out=out_rows[:, :, c * CHUNK : (c + 1) * CHUNK], in_=y[c][:])
            if c < NCHUNK - 1:
                round_y(nc.scalar.copy, c)
        quantise_y(0)
        quantise_y(1)
        nc.sync.dma_start(out=out_words[:, 0:HALF], in_=y_codes[:, 0:HALF].bitcast(I32))
        round_y(nc.vector.tensor_copy, NCHUNK - 1)
        quantise_y(2)
        quantise_y(3)
        nc.sync.dma_start(out=out_words[:, HALF:J], in_=y_codes[:, HALF:J].bitcast(I32))
        for quad in range(4):
            queue = nc.scalar if quad % 2 == 0 else nc.sync
            queue.dma_start(
                out=out_2[0, 4 * quad : 4 * quad + 4, :].bitcast(I32),
                in_=y_plane[32 * quad : 32 * quad + 4, :].bitcast(I32),
            )
